import numpy as np
import ml_dtypes


def mxq(x, axis, fmt="e4m3"):
    dtype, down = {"e4m3": (ml_dtypes.float8_e4m3fn, 7), "e5m2": (ml_dtypes.float8_e5m2, 14)}[fmt]
    v = np.moveaxis(np.asarray(x, np.float32).astype(ml_dtypes.bfloat16).astype(np.float64), axis, -1)
    blocks = v.reshape(v.shape[:-1] + (-1, 32))
    amax = np.abs(blocks).max(-1, keepdims=True)
    byte = np.maximum(np.where(amax > 0, np.frexp(amax)[1] - 1 + 127, 0) - down, 1)
    scale = np.exp2(byte - 127.0)
    codes = (blocks / scale).astype(np.float32).astype(dtype).astype(np.float64)
    return np.moveaxis((codes * scale).reshape(v.shape), -1, axis)


WIDE = False


def mx_kscale(k):
    if not WIDE:
        return np.ones(k)
    levels = np.array([10, -10, 5, -5, 0])
    if k % 512:
        return np.exp2(np.random.permutation(np.resize(levels, k // 32))).repeat(32)
    a = np.empty((k // 512, 16))
    for p in range(k // 512):
        a[p, :8] = np.random.permutation(np.resize(levels, 8))
        for g in range(8):
            far = levels[np.abs(levels - a[p, g]) >= 10]
            a[p, g + 8] = far[np.random.randint(len(far))]
    return np.exp2(a.ravel()).repeat(32)


def f64(x):
    return np.asarray(x).astype(np.float64)


def striped8(idx):
    return np.asarray(idx).reshape(8, -1, 16).transpose(0, 2, 1).reshape(128, -1).astype(np.uint16)


def unstriped8(offs):
    return offs.reshape(8, 16, -1).transpose(0, 2, 1).reshape(8, -1).astype(np.int64)


def pick8(x, idx, run):
    r = np.arange(len(x))
    return x[r[:, None], idx[r % (8 * run) // run]]


E2M1 = np.array([0.0, 0.5, 1.0, 1.5, 2.0, 3.0, 4.0, 6.0, -0.0, -0.5, -1.0, -1.5, -2.0, -3.0, -4.0, -6.0])


def pack_weight(w, fmt):
    k, n = w.shape
    w = f64(np.asarray(w, np.float32).astype(ml_dtypes.bfloat16)).reshape(k // 32, 32, n)
    amax = np.abs(w).max(1)
    if fmt == "e4m3":
        byte = np.frexp(amax)[1] - 1 + 127 - 7
    else:
        mant, ex = np.frexp(amax / 6.0)
        byte = np.where(mant > 0.5, ex, ex - 1) + 127
    byte = np.clip(np.where(amax > 0, byte, 1), 1, 254)
    scaled = (w * np.exp2(127.0 - byte)[:, None, :]).reshape(k, n).astype(np.float32)
    by_word = np.ascontiguousarray(scaled.reshape(k // 512, 128, 4, n).transpose(0, 1, 3, 2))
    if fmt == "e4m3":
        words = by_word.astype(ml_dtypes.float8_e4m3fn).view(np.uint8)
    else:
        c = by_word.astype(ml_dtypes.float4_e2m1fn).view(np.uint8) & 0xF
        words = (c[..., 0::2] | (c[..., 1::2] << 4)).reshape(k // 512, 128, 2 * n)
    return np.ascontiguousarray(words), np.ascontiguousarray(byte.astype(np.uint8).reshape(k // 512, 16, n))


def unpack_weight(words, scales, fmt):
    g, _, n = scales.shape
    words = np.ascontiguousarray(words).reshape(g, 128, n, -1)
    if fmt == "e4m3":
        vals = words.view(ml_dtypes.float8_e4m3fn).astype(np.float64)
    else:
        nib = np.empty((g, 128, n, 4), np.uint8)
        nib[..., 0::2] = words & 0xF
        nib[..., 1::2] = words >> 4
        vals = E2M1[nib]
    vals = vals * np.repeat(np.exp2(scales.astype(np.float64) - 127.0), 8, axis=1)[..., None]
    return vals.transpose(0, 1, 3, 2).reshape(g * 512, n)


D, K, T, U, X, S, I, Q = 512, 512, 1024, 1024, 1024, 1024, 512, 128


def setup_inputs():
    n = np.random.standard_normal
    idx = np.stack([np.random.permutation(T)[:I] for _ in range(8)])
    idx2 = np.stack([np.random.permutation(U)[:I] for _ in range(8)])
    idx3 = np.stack([np.random.permutation(X)[:I] for _ in range(8)])
    idx4 = np.stack([np.random.permutation(S)[:I] for _ in range(8)])
    idx5 = np.stack([np.random.permutation(T)[:I] for _ in range(8)])
    idx6 = np.stack([np.random.permutation(X)[:I] for _ in range(8)])
    fd = mx_kscale(D)
    fk = mx_kscale(K)
    wqp = pack_weight(n((D, K)) * 1.0 / np.sqrt(D) * fd[:, None] * fk, "e4m3")
    keysp = pack_weight(n((K, T)) * 1.0 / np.sqrt(K) / fk[:, None], "e4m3")
    notesp = pack_weight(n((K, U)) * 1.0 / np.sqrt(K) / fk[:, None], "e2m1")
    usersp = pack_weight(n((D, X)) * 1.0 / np.sqrt(D) * fd[:, None], "e4m3")
    shelvesp = pack_weight(n((D, S)) * 1.0 / np.sqrt(D) * fd[:, None], "e2m1")
    return {
        "states": (n((D, Q)) * 0.95 / fd[:, None]).astype(np.float32),
        "wq_words": wqp[0],
        "wq_scales": wqp[1],
        "keys_words": keysp[0],
        "keys_scales": keysp[1],
        "notes_words": notesp[0],
        "notes_scales": notesp[1],
        "users_words": usersp[0],
        "users_scales": usersp[1],
        "shelves_words": shelvesp[0],
        "shelves_scales": shelvesp[1],
        "offs": striped8(idx),
        "offs2": striped8(idx2),
        "offs3": striped8(idx3),
        "offs4": striped8(idx4),
        "offs5": striped8(idx5),
        "offs6": striped8(idx6),
    }


def reference(states, wq_words, wq_scales, keys_words, keys_scales, notes_words, notes_scales, users_words, users_scales, shelves_words, shelves_scales, offs, offs2, offs3, offs4, offs5, offs6):
    idx = unstriped8(offs)
    idx2 = unstriped8(offs2)
    idx3 = unstriped8(offs3)
    idx4 = unstriped8(offs4)
    idx5 = unstriped8(offs5)
    idx6 = unstriped8(offs6)
    wqu = unpack_weight(wq_words, wq_scales, "e4m3")
    keysu = unpack_weight(keys_words, keys_scales, "e4m3")
    notesu = unpack_weight(notes_words, notes_scales, "e2m1")
    usersu = unpack_weight(users_words, users_scales, "e4m3")
    shelvesu = unpack_weight(shelves_words, shelves_scales, "e2m1")
    statesq = mxq(f64(states), 0, "e4m3")
    qv = wqu.T @ statesq
    qvq = mxq(qv, 0, "e4m3")
    a = qvq.T @ keysu
    b = qvq.T @ notesu
    c0 = statesq.T @ usersu
    d0 = statesq.T @ shelvesu
    r = pick8(b, idx2, 16) - pick8(a, idx, 16)
    v = pick8(d0, idx4, 16) - pick8(c0, idx3, 16)
    f1 = np.zeros((Q, T))
    f1[np.arange(Q)[:, None], idx[np.arange(Q) % 128 // 16]] = v
    f2 = np.zeros((Q, X))
    f2[np.arange(Q)[:, None], idx3[np.arange(Q) % 128 // 16]] = r
    aa = a + f1
    cc = c0 + f2
    y = pick8(aa, idx5, 16) - pick8(cc, idx6, 16)
    return y

@@ -1,0 +1,193 @@
+from contextlib import ExitStack
+
+import concourse.mybir as mybir
+from concourse.masks import make_identity
+
+F32 = mybir.dt.float32
+BF16 = mybir.dt.bfloat16
+I32 = mybir.dt.int32
+U32 = mybir.dt.uint32
+U16 = mybir.dt.uint16
+U8 = mybir.dt.uint8
+FP8X4 = mybir.dt.float8_e4m3fn_x4
+FP4X4 = mybir.dt.float4_e2m1fn_x4
+ALU = mybir.AluOpType
+COPY = mybir.ActivationFunctionType.Copy
+
+P = 128
+PACK = 4
+Q = 128
+K = 512
+COLS = 1024
+SLOTS = 512
+BANK = 512
+HALF = SLOTS // 2
+LIST_COLS = SLOTS // 16
+
+FLOPS = 2 * 512 * Q * (K + 4 * COLS)
+
+
+def tile_attend_crossgaps_madefour_kernel(
+    tc, states, wq_words, wq_scales, keys_words, keys_scales, notes_words, notes_scales,
+    users_words, users_scales, shelves_words, shelves_scales,
+    offs, offs2, offs3, offs4, offs5, offs6, out,
+):
+    nc = tc.nc
+    with ExitStack() as ctx:
+        sb = ctx.enter_context(tc.tile_pool(name="sb", bufs=1))
+        ps = ctx.enter_context(tc.psum_pool(name="ps", bufs=1))
+
+        def plane_tile(name, width):
+            plane = sb.tile([P, width], U8, name=name, align_bytes=64)
+            return plane
+
+        def load_rows(plane, scales, quadrants):
+            for g in quadrants:
+                nc.sync.dma_start(
+                    out=plane[32 * g : 32 * g + 4, :].bitcast(I32),
+                    in_=scales[0, 4 * g : 4 * g + 4, :].bitcast(I32),
+                )
+
+        def load_fp8(name, words, width):
+            t = sb.tile([P, width], U32, name=name, align_bytes=64)
+            nc.sync.dma_start(
+                out=t[:].bitcast(I32),
+                in_=words[0].rearrange("p n t -> p (n t)").bitcast(I32),
+            )
+            return t
+
+        def load_fp4(name, words):
+            t = sb.tile([P, 2 * COLS], U8, name=name, align_bytes=64)
+            nc.sync.dma_start(out=t[:].bitcast(I32), in_=words[0].bitcast(I32))
+            return t
+
+        def load_list(name, src):
+            t = sb.tile([P, LIST_COLS], U16, name=name)
+            nc.sync.dma_start(t[:], src)
+            return t
+
+        wq_pl = plane_tile("wq_pl", K)
+        shelves_pl = plane_tile("shelves_pl", COLS)
+        users_pl = plane_tile("users_pl", COLS)
+        f1 = sb.tile([P, COLS], F32, name="f1")
+        f2 = sb.tile([P, COLS], F32, name="f2")
+        nc.vector.memset(f1[:], 0.0)
+        nc.vector.memset(f2[:], 0.0)
+        ident = sb.tile([P, P], F32, name="ident")
+        make_identity(nc, ident[:])
+        keys_pl = plane_tile("keys_pl", COLS)
+        notes_pl = plane_tile("notes_pl", COLS)
+
+        raw = sb.tile([P, PACK, Q], F32, name="raw")
+        nc.sync.dma_start(out=raw[:], in_=states.rearrange("(p j) q -> p j q", j=PACK))
+        load_rows(wq_pl, wq_scales, range(4))
+        load_rows(shelves_pl, shelves_scales, range(1))
+        wq_w = load_fp8("wq_w", wq_words, K)
+        shelves_w = load_fp4("shelves_w", shelves_words)
+        load_rows(shelves_pl, shelves_scales, range(1, 4))
+        users_w = load_fp8("users_w", users_words, COLS)
+        load_rows(users_pl, users_scales, range(4))
+        l4 = load_list("l4", offs4)
+        l3 = load_list("l3", offs3)
+        keys_w = load_fp8("keys_w", keys_words, COLS)
+        l1 = load_list("l1", offs)
+        load_rows(keys_pl, keys_scales, range(4))
+        notes_w = load_fp4("notes_w", notes_words)
+        load_rows(notes_pl, notes_scales, range(1))
+        l2 = load_list("l2", offs2)
+        load_rows(notes_pl, notes_scales, range(1, 4))
+        l5 = load_list("l5", offs5)
+        l6 = load_list("l6", offs6)
+
+        s_bf = sb.tile([P, Q, PACK], BF16, name="s_bf", align_bytes=64)
+        nc.vector.tensor_copy(out=s_bf[:], in_=raw[:].rearrange("p j q -> p q j"))
+        s_codes = sb.tile([P, Q], U32, name="s_codes", align_bytes=64)
+        s_pl = sb.tile([P, Q], U8, name="s_pl", align_bytes=64)
+        nc.vector.quantize_mx(out=s_codes[:].bitcast(FP8X4), scales=s_pl[:],
+                              in_=s_bf[:].rearrange("p q j -> p (q j)"))
+
+        def product(tag, codes, plane, words, words_pl, h, fp4):
+            acc = ps.tile([P, BANK], F32, name="acc", tag=tag)
+            if fp4:
+                rhs = words[:, 2 * BANK * h : 2 * BANK * (h + 1)].bitcast(FP4X4)
+            else:
+                rhs = words[:, BANK * h : BANK * (h + 1)].bitcast(FP8X4)
+            nc.tensor.matmul_mx(out=acc[:], lhsT=codes[:].bitcast(FP8X4), lhsT_scale=plane[:],
+                                rhs=rhs, rhs_scale=words_pl[:, BANK * h : BANK * (h + 1)],
+                                start=True, stop=True)
+            return acc
+
+        qv_ps = product("bank0", s_codes, s_pl, wq_w, wq_pl, 0, False)
+        qv_bf = sb.tile([P, K], BF16, name="qv_bf", align_bytes=64)
+        nc.scalar.activation(
+            out=qv_bf[:].rearrange("p (u m e) -> p u m e", u=2, e=2),
+            in_=qv_ps[:].rearrange("p (m u e) -> p u m e", u=2, e=2), func=COPY)
+        d_ps0 = product("bank2", s_codes, s_pl, shelves_w, shelves_pl, 0, True)
+        turned = ps.tile([P, 2, Q], F32, name="turned", tag="bank1")
+        pairs = qv_bf[:].bitcast(F32)
+        for u in range(2):
+            nc.tensor.transpose(turned[:, u, :], pairs[:, P * u : P * (u + 1)], ident[:])
+        d_ps1 = product("bank3", s_codes, s_pl, shelves_w, shelves_pl, 1, True)
+        c_ps0 = product("bank4", s_codes, s_pl, users_w, users_pl, 0, False)
+        c_ps1 = product("bank5", s_codes, s_pl, users_w, users_pl, 1, False)
+
+        d0 = sb.tile([P, COLS], F32, name="d0")
+        c0 = sb.tile([P, COLS], F32, name="c0")
+        a = sb.tile([P, COLS], F32, name="a")
+        b = sb.tile([P, COLS], F32, name="b")
+        lo, hi = slice(0, BANK), slice(BANK, COLS)
+
+        nc.vector.tensor_copy(out=d0[:, lo], in_=d_ps0[:])
+        q_bf = sb.tile([P, Q * PACK], BF16, name="q_bf", align_bytes=64)
+        nc.scalar.copy(out=q_bf[:].bitcast(F32).rearrange("p (q u) -> p q u", u=2),
+                       in_=turned[:].rearrange("p u q -> p q u"))
+        q_codes = sb.tile([P, Q], U32, name="q_codes", align_bytes=64)
+        q_pl = sb.tile([P, Q], U8, name="q_pl", align_bytes=64)
+        nc.vector.quantize_mx(out=q_codes[:].bitcast(FP8X4), scales=q_pl[:], in_=q_bf[:])
+        nc.scalar.copy(out=d0[:, hi], in_=d_ps1[:])
+        nc.vector.tensor_copy(out=c0[:, lo], in_=c_ps0[:])
+        nc.scalar.copy(out=c0[:, hi], in_=c_ps1[:])
+
+        a_ps = [product("bank%d" % h, q_codes, q_pl, keys_w, keys_pl, h, False) for h in range(2)]
+        b_ps = [product("bank%d" % (6 + h), q_codes, q_pl, notes_w, notes_pl, h, True) for h in range(2)]
+
+        def part(lst, h):
+            return lst[:, (HALF // 16) * h : (HALF // 16) * (h + 1)]
+
+        def scalar_gather(name, window, lst, h, sign):
+            g = sb.tile([P, HALF], F32, name="g", tag=name)
+            nc.scalar.activation(out=g[:], in_=window[:].indirect(part(lst, h)), func=COPY, scale=sign)
+            return g
+
+        def vector_gather(name, window, lst, h):
+            g = sb.tile([P, HALF], F32, name=name)
+            nc.vector.tensor_copy(out=g[:], in_=window[:].indirect(part(lst, h)))
+            return g
+
+        dg0 = vector_gather("dg0", d0, l4, 0)
+        cn0 = scalar_gather("cn0", c0, l3, 0, -1.0)
+        nc.vector.tensor_tensor(f1[:].indirect(part(l1, 0)), dg0[:], cn0[:], ALU.add)
+        dg1 = scalar_gather("dg1", d0, l4, 1, 1.0)
+        cn1 = scalar_gather("cn1", c0, l3, 1, -1.0)
+        nc.vector.tensor_tensor(f1[:].indirect(part(l1, 1)), dg1[:], cn1[:], ALU.add)
+
+        for dst, banks in ((a, a_ps), (b, b_ps)):
+            nc.scalar.copy(out=dst[:, lo], in_=banks[0][:])
+            nc.scalar.copy(out=dst[:, hi], in_=banks[1][:])
+        aa = sb.tile([P, COLS], F32, name="aa")
+        nc.vector.tensor_tensor(aa[:], a[:], f1[:], ALU.add)
+
+        for h in range(2):
+            an = scalar_gather("an%d" % h, a, l1, h, -1.0)
+            bg = scalar_gather("bg%d" % h, b, l2, h, 1.0)
+            nc.vector.tensor_tensor(f2[:].indirect(part(l3, h)), bg[:], an[:], ALU.add)
+        ag = [scalar_gather(tag, aa, l5, h, 1.0) for h, tag in enumerate(("an0", "bg0"))]
+        cc = sb.tile([P, COLS], F32, name="cc")
+        nc.vector.tensor_tensor(cc[:], c0[:], f2[:], ALU.add)
+
+        cg = [scalar_gather("cg0", cc, l6, 0, 1.0), vector_gather("cg1", cc, l6, 1)]
+        for h in range(2):
+            y = sb.tile([P, HALF], F32, name="y%d" % h)
+            nc.vector.tensor_tensor(y[:], ag[h][:], cg[h][:], ALU.subtract)
+            queue = nc.sync if h == 0 else nc.scalar
+            queue.dma_start(out=out[:, HALF * h : HALF * (h + 1)], in_=y[:])

@@ -1,7 +1,6 @@
 from contextlib import ExitStack
 
 import concourse.mybir as mybir
-from concourse.masks import make_identity
 
 F32 = mybir.dt.float32
 BF16 = mybir.dt.bfloat16
@@ -23,6 +22,8 @@ SLOTS = 512
 BANK = 512
 HALF = SLOTS // 2
 LIST_COLS = SLOTS // 16
+CAST_SPLIT = 72
+DEAL_SPLIT = 20
 
 FLOPS = 2 * 512 * Q * (K + 4 * COLS)
 
@@ -38,12 +39,12 @@ def tile_attend_crossgaps_madefour_kernel(
         ps = ctx.enter_context(tc.psum_pool(name="ps", bufs=1))
 
         def plane_tile(name, width):
-            plane = sb.tile([P, width], U8, name=name, align_bytes=64)
+            plane = sb.tile([P, width], U8, name="plane", tag=name, align_bytes=64)
             return plane
 
-        def load_rows(plane, scales, quadrants):
+        def load_rows(plane, scales, quadrants, queue=nc.sync):
             for g in quadrants:
-                nc.sync.dma_start(
+                queue.dma_start(
                     out=plane[32 * g : 32 * g + 4, :].bitcast(I32),
                     in_=scales[0, 4 * g : 4 * g + 4, :].bitcast(I32),
                 )
@@ -57,7 +58,7 @@ def tile_attend_crossgaps_madefour_kernel(
             return t
 
         def load_fp4(name, words):
-            t = sb.tile([P, 2 * COLS], U8, name=name, align_bytes=64)
+            t = sb.tile([P, 2 * COLS], U8, name="t", tag=name, align_bytes=64)
             nc.sync.dma_start(out=t[:].bitcast(I32), in_=words[0].bitcast(I32))
             return t
 
@@ -67,16 +68,16 @@ def tile_attend_crossgaps_madefour_kernel(
             return t
 
         wq_pl = plane_tile("wq_pl", K)
+        nc.gpsimd.memset(wq_pl[:].bitcast(I32), 0)
         shelves_pl = plane_tile("shelves_pl", COLS)
         users_pl = plane_tile("users_pl", COLS)
         f1 = sb.tile([P, COLS], F32, name="f1")
         f2 = sb.tile([P, COLS], F32, name="f2")
         nc.vector.memset(f1[:], 0.0)
         nc.vector.memset(f2[:], 0.0)
-        ident = sb.tile([P, P], F32, name="ident")
-        make_identity(nc, ident[:])
         keys_pl = plane_tile("keys_pl", COLS)
         notes_pl = plane_tile("notes_pl", COLS)
+        load_rows(notes_pl, notes_scales, range(4), nc.gpsimd)
 
         raw = sb.tile([P, PACK, Q], F32, name="raw")
         nc.sync.dma_start(out=raw[:], in_=states.rearrange("(p j) q -> p j q", j=PACK))
@@ -92,15 +93,15 @@ def tile_attend_crossgaps_madefour_kernel(
         keys_w = load_fp8("keys_w", keys_words, COLS)
         l1 = load_list("l1", offs)
         load_rows(keys_pl, keys_scales, range(4))
-        notes_w = load_fp4("notes_w", notes_words)
-        load_rows(notes_pl, notes_scales, range(1))
         l2 = load_list("l2", offs2)
-        load_rows(notes_pl, notes_scales, range(1, 4))
+        notes_w = load_fp4("notes_w", notes_words)
         l5 = load_list("l5", offs5)
         l6 = load_list("l6", offs6)
 
         s_bf = sb.tile([P, Q, PACK], BF16, name="s_bf", align_bytes=64)
-        nc.vector.tensor_copy(out=s_bf[:], in_=raw[:].rearrange("p j q -> p q j"))
+        by_row = raw[:].rearrange("p j q -> p q j")
+        nc.vector.tensor_copy(out=s_bf[:, :CAST_SPLIT, :], in_=by_row[:, :CAST_SPLIT, :])
+        nc.scalar.activation(out=s_bf[:, CAST_SPLIT:, :], in_=by_row[:, CAST_SPLIT:, :], func=COPY)
         s_codes = sb.tile([P, Q], U32, name="s_codes", align_bytes=64)
         s_pl = sb.tile([P, Q], U8, name="s_pl", align_bytes=64)
         nc.vector.quantize_mx(out=s_codes[:].bitcast(FP8X4), scales=s_pl[:],
@@ -117,16 +118,24 @@ def tile_attend_crossgaps_madefour_kernel(
                                 start=True, stop=True)
             return acc
 
-        qv_ps = product("bank0", s_codes, s_pl, wq_w, wq_pl, 0, False)
-        qv_bf = sb.tile([P, K], BF16, name="qv_bf", align_bytes=64)
-        nc.scalar.activation(
-            out=qv_bf[:].rearrange("p (u m e) -> p u m e", u=2, e=2),
-            in_=qv_ps[:].rearrange("p (m u e) -> p u m e", u=2, e=2), func=COPY)
+        wq_dealt = sb.tile([P, K], U32, name="wq_dealt", align_bytes=64)
+        wq_pl_dealt = sb.tile([P, K], U8, name="wq_pl_dealt", align_bytes=64)
+        nc.vector.tensor_copy(out=wq_pl_dealt[:].rearrange("p (j m) -> p j m", j=PACK),
+                              in_=wq_pl[:].rearrange("p (m j) -> p j m", j=PACK))
+        deal = "p (j c i) -> p c j i", "p (c i j) -> p c j i"
+        nc.scalar.copy(out=wq_dealt[:].rearrange(deal[0], j=PACK, i=4)[:, :DEAL_SPLIT],
+                       in_=wq_w[:].rearrange(deal[1], j=PACK, i=4)[:, :DEAL_SPLIT])
+        nc.vector.tensor_copy(
+            out=wq_dealt[:].bitcast(I32).rearrange(deal[0], j=PACK, i=4)[:, DEAL_SPLIT:],
+            in_=wq_w[:].bitcast(I32).rearrange(deal[1], j=PACK, i=4)[:, DEAL_SPLIT:])
+        qv_ps = ps.tile([P, PACK, Q], F32, name="qv_ps", tag="bank0")
+        for j in range(PACK):
+            nc.tensor.matmul_mx(out=qv_ps[:, j, :],
+                                lhsT=wq_dealt[:, P * j : P * (j + 1)].bitcast(FP8X4),
+                                lhsT_scale=wq_pl_dealt[:, P * j : P * (j + 1)],
+                                rhs=s_codes[:].bitcast(FP8X4), rhs_scale=s_pl[:],
+                                start=True, stop=True)
         d_ps0 = product("bank2", s_codes, s_pl, shelves_w, shelves_pl, 0, True)
-        turned = ps.tile([P, 2, Q], F32, name="turned", tag="bank1")
-        pairs = qv_bf[:].bitcast(F32)
-        for u in range(2):
-            nc.tensor.transpose(turned[:, u, :], pairs[:, P * u : P * (u + 1)], ident[:])
         d_ps1 = product("bank3", s_codes, s_pl, shelves_w, shelves_pl, 1, True)
         c_ps0 = product("bank4", s_codes, s_pl, users_w, users_pl, 0, False)
         c_ps1 = product("bank5", s_codes, s_pl, users_w, users_pl, 1, False)
@@ -137,13 +146,13 @@ def tile_attend_crossgaps_madefour_kernel(
         b = sb.tile([P, COLS], F32, name="b")
         lo, hi = slice(0, BANK), slice(BANK, COLS)
 
-        nc.vector.tensor_copy(out=d0[:, lo], in_=d_ps0[:])
         q_bf = sb.tile([P, Q * PACK], BF16, name="q_bf", align_bytes=64)
-        nc.scalar.copy(out=q_bf[:].bitcast(F32).rearrange("p (q u) -> p q u", u=2),
-                       in_=turned[:].rearrange("p u q -> p q u"))
+        nc.scalar.activation(out=q_bf[:].rearrange("p (q j) -> p q j", j=PACK),
+                             in_=qv_ps[:].rearrange("p j q -> p q j"), func=COPY)
         q_codes = sb.tile([P, Q], U32, name="q_codes", align_bytes=64)
         q_pl = sb.tile([P, Q], U8, name="q_pl", align_bytes=64)
         nc.vector.quantize_mx(out=q_codes[:].bitcast(FP8X4), scales=q_pl[:], in_=q_bf[:])
+        nc.scalar.copy(out=d0[:, lo], in_=d_ps0[:])
         nc.scalar.copy(out=d0[:, hi], in_=d_ps1[:])
         nc.vector.tensor_copy(out=c0[:, lo], in_=c_ps0[:])
         nc.scalar.copy(out=c0[:, hi], in_=c_ps1[:])
@@ -155,7 +164,7 @@ def tile_attend_crossgaps_madefour_kernel(
             return lst[:, (HALF // 16) * h : (HALF // 16) * (h + 1)]
 
         def scalar_gather(name, window, lst, h, sign):
-            g = sb.tile([P, HALF], F32, name="g", tag=name)
+            g = sb.tile([P, HALF], F32, name="g", tag=name, align_bytes=64)
             nc.scalar.activation(out=g[:], in_=window[:].indirect(part(lst, h)), func=COPY, scale=sign)
             return g
 
@@ -164,24 +173,23 @@ def tile_attend_crossgaps_madefour_kernel(
             nc.vector.tensor_copy(out=g[:], in_=window[:].indirect(part(lst, h)))
             return g
 
-        dg0 = vector_gather("dg0", d0, l4, 0)
-        cn0 = scalar_gather("cn0", c0, l3, 0, -1.0)
-        nc.vector.tensor_tensor(f1[:].indirect(part(l1, 0)), dg0[:], cn0[:], ALU.add)
-        dg1 = scalar_gather("dg1", d0, l4, 1, 1.0)
-        cn1 = scalar_gather("cn1", c0, l3, 1, -1.0)
-        nc.vector.tensor_tensor(f1[:].indirect(part(l1, 1)), dg1[:], cn1[:], ALU.add)
+        dg = [vector_gather("dg%d" % h, d0, l4, h) for h in range(2)]
+        for h in range(2):
+            cn = scalar_gather("cn%d" % h, c0, l3, h, -1.0)
+            nc.vector.tensor_tensor(f1[:].indirect(part(l1, h)), dg[h][:], cn[:], ALU.add)
 
         for dst, banks in ((a, a_ps), (b, b_ps)):
             nc.scalar.copy(out=dst[:, lo], in_=banks[0][:])
             nc.scalar.copy(out=dst[:, hi], in_=banks[1][:])
-        aa = sb.tile([P, COLS], F32, name="aa")
+        an0 = scalar_gather("notes_w", a, l1, 0, -1.0)
+        bg0 = scalar_gather("bg0", b, l2, 0, 1.0)
+        nc.vector.tensor_tensor(f2[:].indirect(part(l3, 0)), bg0[:], an0[:], ALU.add)
+        aa = sb.tile([P, COLS], F32, name="aa", tag="bg0", align_bytes=64)
         nc.vector.tensor_tensor(aa[:], a[:], f1[:], ALU.add)
-
-        for h in range(2):
-            an = scalar_gather("an%d" % h, a, l1, h, -1.0)
-            bg = scalar_gather("bg%d" % h, b, l2, h, 1.0)
-            nc.vector.tensor_tensor(f2[:].indirect(part(l3, h)), bg[:], an[:], ALU.add)
-        ag = [scalar_gather(tag, aa, l5, h, 1.0) for h, tag in enumerate(("an0", "bg0"))]
+        an1 = scalar_gather("notes_pl", a, l1, 1, -1.0)
+        bg1 = scalar_gather("bg1", b, l2, 1, 1.0)
+        nc.vector.tensor_tensor(f2[:].indirect(part(l3, 1)), bg1[:], an1[:], ALU.add)
+        ag = [scalar_gather("ag%d" % h, aa, l5, h, 1.0) for h in range(2)]
         cc = sb.tile([P, COLS], F32, name="cc")
         nc.vector.tensor_tensor(cc[:], c0[:], f2[:], ALU.add)
 

@@ -1,6 +1,7 @@
 from contextlib import ExitStack
 
 import concourse.mybir as mybir
+from concourse.masks import make_identity
 
 F32 = mybir.dt.float32
 BF16 = mybir.dt.bfloat16
@@ -24,6 +25,8 @@ HALF = SLOTS // 2
 LIST_COLS = SLOTS // 16
 CAST_SPLIT = 72
 DEAL_SPLIT = 20
+ADD_SPLIT = 800
+BLOCKS = BANK // P
 
 FLOPS = 2 * 512 * Q * (K + 4 * COLS)
 
@@ -78,6 +81,8 @@ def tile_attend_crossgaps_madefour_kernel(
         keys_pl = plane_tile("keys_pl", COLS)
         notes_pl = plane_tile("notes_pl", COLS)
         load_rows(notes_pl, notes_scales, range(4), nc.gpsimd)
+        ident = sb.tile([P, P], F32, name="ident")
+        make_identity(nc, ident[:])
 
         raw = sb.tile([P, PACK, Q], F32, name="raw")
         nc.sync.dma_start(out=raw[:], in_=states.rearrange("(p j) q -> p j q", j=PACK))
@@ -143,7 +148,7 @@ def tile_attend_crossgaps_madefour_kernel(
         d0 = sb.tile([P, COLS], F32, name="d0")
         c0 = sb.tile([P, COLS], F32, name="c0")
         a = sb.tile([P, COLS], F32, name="a")
-        b = sb.tile([P, COLS], F32, name="b")
+        b = sb.tile([P, COLS], F32, name="b", tag="b")
         lo, hi = slice(0, BANK), slice(BANK, COLS)
 
         q_bf = sb.tile([P, Q * PACK], BF16, name="q_bf", align_bytes=64)
@@ -184,16 +189,34 @@ def tile_attend_crossgaps_madefour_kernel(
         an0 = scalar_gather("notes_w", a, l1, 0, -1.0)
         bg0 = scalar_gather("bg0", b, l2, 0, 1.0)
         nc.vector.tensor_tensor(f2[:].indirect(part(l3, 0)), bg0[:], an0[:], ALU.add)
-        aa = sb.tile([P, COLS], F32, name="aa", tag="bg0", align_bytes=64)
-        nc.vector.tensor_tensor(aa[:], a[:], f1[:], ALU.add)
         an1 = scalar_gather("notes_pl", a, l1, 1, -1.0)
         bg1 = scalar_gather("bg1", b, l2, 1, 1.0)
         nc.vector.tensor_tensor(f2[:].indirect(part(l3, 1)), bg1[:], an1[:], ALU.add)
+        aa = sb.tile([P, COLS], F32, name="aa", tag="aa", align_bytes=64)
+        aa_t = sb.tile([P, COLS], F32, name="aa_t", tag="b")
+        sums = [ps.tile([P, BANK], F32, name="sums", tag="bank%d" % (6 + h)) for h in range(2)]
+        for first, term in ((True, a), (False, f1)):
+            for h in range(2):
+                for blk in range(BLOCKS):
+                    src = slice(BANK * h + P * blk, BANK * h + P * (blk + 1))
+                    nc.tensor.matmul(sums[h][:, P * blk : P * (blk + 1)], lhsT=term[:, src], rhs=ident[:],
+                                     is_transpose=True, start=first and blk == 0,
+                                     stop=not first and blk == BLOCKS - 1)
+        for h, cols in enumerate((lo, hi)):
+            nc.scalar.copy(out=aa_t[:, cols], in_=sums[h][:])
+        for h, cols in enumerate((lo, hi)):
+            acc = ps.tile([P, BANK], F32, name="acc", tag="bank%d" % h)
+            for blk in range(BANK // P):
+                src = slice(BANK * h + P * blk, BANK * h + P * (blk + 1))
+                nc.tensor.transpose(acc[:, P * blk : P * (blk + 1)], aa_t[:, src], ident[:])
+            nc.scalar.copy(out=aa[:, cols], in_=acc[:])
         ag = [scalar_gather("ag%d" % h, aa, l5, h, 1.0) for h in range(2)]
         cc = sb.tile([P, COLS], F32, name="cc")
-        nc.vector.tensor_tensor(cc[:], c0[:], f2[:], ALU.add)
+        nc.vector.tensor_tensor(cc[:, lo], c_ps0[:], f2[:, lo], ALU.add)
+        nc.vector.tensor_tensor(cc[:, BANK:ADD_SPLIT], c_ps1[:, : ADD_SPLIT - BANK], f2[:, BANK:ADD_SPLIT], ALU.add)
+        nc.gpsimd.tensor_tensor(cc[:, ADD_SPLIT:], c0[:, ADD_SPLIT:], f2[:, ADD_SPLIT:], ALU.add)
 
-        cg = [scalar_gather("cg0", cc, l6, 0, 1.0), vector_gather("cg1", cc, l6, 1)]
+        cg = [scalar_gather("aa", cc, l6, 0, 1.0), vector_gather("cg1", cc, l6, 1)]
         for h in range(2):
             y = sb.tile([P, HALF], F32, name="y%d" % h)
             nc.vector.tensor_tensor(y[:], ag[h][:], cg[h][:], ALU.subtract)

@@ -192,7 +192,7 @@ def tile_attend_crossgaps_madefour_kernel(
         an1 = scalar_gather("notes_pl", a, l1, 1, -1.0)
         bg1 = scalar_gather("bg1", b, l2, 1, 1.0)
         nc.vector.tensor_tensor(f2[:].indirect(part(l3, 1)), bg1[:], an1[:], ALU.add)
-        aa = sb.tile([P, COLS], F32, name="aa", tag="aa", align_bytes=64)
+        aa = sb.tile([P, COLS], F32, name="aa")
         aa_t = sb.tile([P, COLS], F32, name="aa_t", tag="b")
         sums = [ps.tile([P, BANK], F32, name="sums", tag="bank%d" % (6 + h)) for h in range(2)]
         for first, term in ((True, a), (False, f1)):
@@ -216,7 +216,7 @@ def tile_attend_crossgaps_madefour_kernel(
         nc.vector.tensor_tensor(cc[:, BANK:ADD_SPLIT], c_ps1[:, : ADD_SPLIT - BANK], f2[:, BANK:ADD_SPLIT], ALU.add)
         nc.gpsimd.tensor_tensor(cc[:, ADD_SPLIT:], c0[:, ADD_SPLIT:], f2[:, ADD_SPLIT:], ALU.add)
 
-        cg = [scalar_gather("aa", cc, l6, 0, 1.0), vector_gather("cg1", cc, l6, 1)]
+        cg = [vector_gather("cg%d" % h, cc, l6, h) for h in range(2)]
         for h in range(2):
             y = sb.tile([P, HALF], F32, name="y%d" % h)
             nc.vector.tensor_tensor(y[:], ag[h][:], cg[h][:], ALU.subtract)

from contextlib import ExitStack

import concourse.mybir as mybir
from concourse.masks import make_identity

F32 = mybir.dt.float32
BF16 = mybir.dt.bfloat16
I32 = mybir.dt.int32
U32 = mybir.dt.uint32
U16 = mybir.dt.uint16
U8 = mybir.dt.uint8
FP8X4 = mybir.dt.float8_e4m3fn_x4
FP4X4 = mybir.dt.float4_e2m1fn_x4
ALU = mybir.AluOpType
COPY = mybir.ActivationFunctionType.Copy

P = 128
PACK = 4
Q = 128
K = 512
COLS = 1024
SLOTS = 512
BANK = 512
HALF = SLOTS // 2
LIST_COLS = SLOTS // 16
CAST_SPLIT = 72
DEAL_SPLIT = 20
ADD_SPLIT = 800
BLOCKS = BANK // P

FLOPS = 2 * 512 * Q * (K + 4 * COLS)


def tile_attend_crossgaps_madefour_kernel(
    tc, states, wq_words, wq_scales, keys_words, keys_scales, notes_words, notes_scales,
    users_words, users_scales, shelves_words, shelves_scales,
    offs, offs2, offs3, offs4, offs5, offs6, out,
):
    nc = tc.nc
    with ExitStack() as ctx:
        sb = ctx.enter_context(tc.tile_pool(name="sb", bufs=1))
        ps = ctx.enter_context(tc.psum_pool(name="ps", bufs=1))

        def plane_tile(name, width):
            plane = sb.tile([P, width], U8, name="plane", tag=name, align_bytes=64)
            return plane

        def load_rows(plane, scales, quadrants, queue=nc.sync):
            for g in quadrants:
                queue.dma_start(
                    out=plane[32 * g : 32 * g + 4, :].bitcast(I32),
                    in_=scales[0, 4 * g : 4 * g + 4, :].bitcast(I32),
                )

        def load_fp8(name, words, width):
            t = sb.tile([P, width], U32, name=name, align_bytes=64)
            nc.sync.dma_start(
                out=t[:].bitcast(I32),
                in_=words[0].rearrange("p n t -> p (n t)").bitcast(I32),
            )
            return t

        def load_fp4(name, words):
            t = sb.tile([P, 2 * COLS], U8, name="t", tag=name, align_bytes=64)
            nc.sync.dma_start(out=t[:].bitcast(I32), in_=words[0].bitcast(I32))
            return t

        def load_list(name, src):
            t = sb.tile([P, LIST_COLS], U16, name=name)
            nc.sync.dma_start(t[:], src)
            return t

        wq_pl = plane_tile("wq_pl", K)
        nc.gpsimd.memset(wq_pl[:].bitcast(I32), 0)
        shelves_pl = plane_tile("shelves_pl", COLS)
        users_pl = plane_tile("users_pl", COLS)
        f1 = sb.tile([P, COLS], F32, name="f1")
        f2 = sb.tile([P, COLS], F32, name="f2")
        nc.vector.memset(f1[:], 0.0)
        nc.vector.memset(f2[:], 0.0)
        keys_pl = plane_tile("keys_pl", COLS)
        notes_pl = plane_tile("notes_pl", COLS)
        load_rows(notes_pl, notes_scales, range(4), nc.gpsimd)
        ident = sb.tile([P, P], F32, name="ident")
        make_identity(nc, ident[:])

        raw = sb.tile([P, PACK, Q], F32, name="raw")
        nc.sync.dma_start(out=raw[:], in_=states.rearrange("(p j) q -> p j q", j=PACK))
        load_rows(wq_pl, wq_scales, range(4))
        load_rows(shelves_pl, shelves_scales, range(1))
        wq_w = load_fp8("wq_w", wq_words, K)
        shelves_w = load_fp4("shelves_w", shelves_words)
        load_rows(shelves_pl, shelves_scales, range(1, 4))
        users_w = load_fp8("users_w", users_words, COLS)
        load_rows(users_pl, users_scales, range(4))
        l4 = load_list("l4", offs4)
        l3 = load_list("l3", offs3)
        keys_w = load_fp8("keys_w", keys_words, COLS)
        l1 = load_list("l1", offs)
        load_rows(keys_pl, keys_scales, range(4))
        l2 = load_list("l2", offs2)
        notes_w = load_fp4("notes_w", notes_words)
        l5 = load_list("l5", offs5)
        l6 = load_list("l6", offs6)

        s_bf = sb.tile([P, Q, PACK], BF16, name="s_bf", align_bytes=64)
        by_row = raw[:].rearrange("p j q -> p q j")
        nc.vector.tensor_copy(out=s_bf[:, :CAST_SPLIT, :], in_=by_row[:, :CAST_SPLIT, :])
        nc.scalar.activation(out=s_bf[:, CAST_SPLIT:, :], in_=by_row[:, CAST_SPLIT:, :], func=COPY)
        s_codes = sb.tile([P, Q], U32, name="s_codes", align_bytes=64)
        s_pl = sb.tile([P, Q], U8, name="s_pl", align_bytes=64)
        nc.vector.quantize_mx(out=s_codes[:].bitcast(FP8X4), scales=s_pl[:],
                              in_=s_bf[:].rearrange("p q j -> p (q j)"))

        def product(tag, codes, plane, words, words_pl, h, fp4):
            acc = ps.tile([P, BANK], F32, name="acc", tag=tag)
            if fp4:
                rhs = words[:, 2 * BANK * h : 2 * BANK * (h + 1)].bitcast(FP4X4)
            else:
                rhs = words[:, BANK * h : BANK * (h + 1)].bitcast(FP8X4)
            nc.tensor.matmul_mx(out=acc[:], lhsT=codes[:].bitcast(FP8X4), lhsT_scale=plane[:],
                                rhs=rhs, rhs_scale=words_pl[:, BANK * h : BANK * (h + 1)],
                                start=True, stop=True)
            return acc

        wq_dealt = sb.tile([P, K], U32, name="wq_dealt", align_bytes=64)
        wq_pl_dealt = sb.tile([P, K], U8, name="wq_pl_dealt", align_bytes=64)
        nc.vector.tensor_copy(out=wq_pl_dealt[:].rearrange("p (j m) -> p j m", j=PACK),
                              in_=wq_pl[:].rearrange("p (m j) -> p j m", j=PACK))
        deal = "p (j c i) -> p c j i", "p (c i j) -> p c j i"
        nc.scalar.copy(out=wq_dealt[:].rearrange(deal[0], j=PACK, i=4)[:, :DEAL_SPLIT],
                       in_=wq_w[:].rearrange(deal[1], j=PACK, i=4)[:, :DEAL_SPLIT])
        nc.vector.tensor_copy(
            out=wq_dealt[:].bitcast(I32).rearrange(deal[0], j=PACK, i=4)[:, DEAL_SPLIT:],
            in_=wq_w[:].bitcast(I32).rearrange(deal[1], j=PACK, i=4)[:, DEAL_SPLIT:])
        qv_ps = ps.tile([P, PACK, Q], F32, name="qv_ps", tag="bank0")
        for j in range(PACK):
            nc.tensor.matmul_mx(out=qv_ps[:, j, :],
                                lhsT=wq_dealt[:, P * j : P * (j + 1)].bitcast(FP8X4),
                                lhsT_scale=wq_pl_dealt[:, P * j : P * (j + 1)],
                                rhs=s_codes[:].bitcast(FP8X4), rhs_scale=s_pl[:],
                                start=True, stop=True)
        d_ps0 = product("bank2", s_codes, s_pl, shelves_w, shelves_pl, 0, True)
        d_ps1 = product("bank3", s_codes, s_pl, shelves_w, shelves_pl, 1, True)
        c_ps0 = product("bank4", s_codes, s_pl, users_w, users_pl, 0, False)
        c_ps1 = product("bank5", s_codes, s_pl, users_w, users_pl, 1, False)

        d0 = sb.tile([P, COLS], F32, name="d0")
        c0 = sb.tile([P, COLS], F32, name="c0")
        a = sb.tile([P, COLS], F32, name="a")
        b = sb.tile([P, COLS], F32, name="b", tag="b")
        lo, hi = slice(0, BANK), slice(BANK, COLS)

        q_bf = sb.tile([P, Q * PACK], BF16, name="q_bf", align_bytes=64)
        nc.scalar.activation(out=q_bf[:].rearrange("p (q j) -> p q j", j=PACK),
                             in_=qv_ps[:].rearrange("p j q -> p q j"), func=COPY)
        q_codes = sb.tile([P, Q], U32, name="q_codes", align_bytes=64)
        q_pl = sb.tile([P, Q], U8, name="q_pl", align_bytes=64)
        nc.vector.quantize_mx(out=q_codes[:].bitcast(FP8X4), scales=q_pl[:], in_=q_bf[:])
        nc.scalar.copy(out=d0[:, lo], in_=d_ps0[:])
        nc.scalar.copy(out=d0[:, hi], in_=d_ps1[:])
        nc.vector.tensor_copy(out=c0[:, lo], in_=c_ps0[:])
        nc.scalar.copy(out=c0[:, hi], in_=c_ps1[:])

        a_ps = [product("bank%d" % h, q_codes, q_pl, keys_w, keys_pl, h, False) for h in range(2)]
        b_ps = [product("bank%d" % (6 + h), q_codes, q_pl, notes_w, notes_pl, h, True) for h in range(2)]

        def part(lst, h):
            return lst[:, (HALF // 16) * h : (HALF // 16) * (h + 1)]

        def scalar_gather(name, window, lst, h, sign):
            g = sb.tile([P, HALF], F32, name="g", tag=name, align_bytes=64)
            nc.scalar.activation(out=g[:], in_=window[:].indirect(part(lst, h)), func=COPY, scale=sign)
            return g

        def vector_gather(name, window, lst, h):
            g = sb.tile([P, HALF], F32, name=name)
            nc.vector.tensor_copy(out=g[:], in_=window[:].indirect(part(lst, h)))
            return g

        dg = [vector_gather("dg%d" % h, d0, l4, h) for h in range(2)]
        for h in range(2):
            cn = scalar_gather("cn%d" % h, c0, l3, h, -1.0)
            nc.vector.tensor_tensor(f1[:].indirect(part(l1, h)), dg[h][:], cn[:], ALU.add)

        for dst, banks in ((a, a_ps), (b, b_ps)):
            nc.scalar.copy(out=dst[:, lo], in_=banks[0][:])
            nc.scalar.copy(out=dst[:, hi], in_=banks[1][:])
        an0 = scalar_gather("notes_w", a, l1, 0, -1.0)
        bg0 = scalar_gather("bg0", b, l2, 0, 1.0)
        nc.vector.tensor_tensor(f2[:].indirect(part(l3, 0)), bg0[:], an0[:], ALU.add)
        an1 = scalar_gather("notes_pl", a, l1, 1, -1.0)
        bg1 = scalar_gather("bg1", b, l2, 1, 1.0)
        nc.vector.tensor_tensor(f2[:].indirect(part(l3, 1)), bg1[:], an1[:], ALU.add)
        aa = sb.tile([P, COLS], F32, name="aa")
        aa_t = sb.tile([P, COLS], F32, name="aa_t", tag="b")
        sums = [ps.tile([P, BANK], F32, name="sums", tag="bank%d" % (6 + h)) for h in range(2)]
        for first, term in ((True, a), (False, f1)):
            for h in range(2):
                for blk in range(BLOCKS):
                    src = slice(BANK * h + P * blk, BANK * h + P * (blk + 1))
                    nc.tensor.matmul(sums[h][:, P * blk : P * (blk + 1)], lhsT=term[:, src], rhs=ident[:],
                                     is_transpose=True, start=first and blk == 0,
                                     stop=not first and blk == BLOCKS - 1)
        for h, cols in enumerate((lo, hi)):
            nc.scalar.copy(out=aa_t[:, cols], in_=sums[h][:])
        for h, cols in enumerate((lo, hi)):
            acc = ps.tile([P, BANK], F32, name="acc", tag="bank%d" % h)
            for blk in range(BANK // P):
                src = slice(BANK * h + P * blk, BANK * h + P * (blk + 1))
                nc.tensor.transpose(acc[:, P * blk : P * (blk + 1)], aa_t[:, src], ident[:])
            nc.scalar.copy(out=aa[:, cols], in_=acc[:])
        ag = [scalar_gather("ag%d" % h, aa, l5, h, 1.0) for h in range(2)]
        cc = sb.tile([P, COLS], F32, name="cc")
        nc.vector.tensor_tensor(cc[:, lo], c_ps0[:], f2[:, lo], ALU.add)
        nc.vector.tensor_tensor(cc[:, BANK:ADD_SPLIT], c_ps1[:, : ADD_SPLIT - BANK], f2[:, BANK:ADD_SPLIT], ALU.add)
        nc.gpsimd.tensor_tensor(cc[:, ADD_SPLIT:], c0[:, ADD_SPLIT:], f2[:, ADD_SPLIT:], ALU.add)

        cg = [vector_gather("cg%d" % h, cc, l6, h) for h in range(2)]
        for h in range(2):
            y = sb.tile([P, HALF], F32, name="y%d" % h)
            nc.vector.tensor_tensor(y[:], ag[h][:], cg[h][:], ALU.subtract)
            queue = nc.sync if h == 0 else nc.scalar
            queue.dma_start(out=out[:, HALF * h : HALF * (h + 1)], in_=y[:])
